import numpy as np, ml_dtypes
CORES = [4,20,36,52,68,84,100,116,132,148,164,180,196,212,228,244]
N = 16
GR, GC, TK = 4, 4, 128
RA = [[-2,1,-2,-1],[-1,2,-2,2],[-2,-1,2,2],[-1,2,-2,1]]
CB = [[1,1,-1,-1],[-1,2,2,2],[-1,1,-1,1],[-2,1,-2,2]]
def setup_inputs(rng):
    return {"x": rng.standard_normal((N, 128, TK), dtype=np.float32).astype(ml_dtypes.bfloat16), "a": (rng.standard_normal((N, 128, 128), dtype=np.float32) / 11).astype(ml_dtypes.bfloat16)}
def setup_inputs_big(rng):
    d = setup_inputs(rng)
    for k in ("x", "a"): d[k] = (d[k].astype(np.float32) * 1024.0).astype(d[k].dtype)
    return d
def setup_inputs_small(rng):
    d = setup_inputs(rng)
    for k in ("x", "a"): d[k] = (d[k].astype(np.float32) * (1 / 1024.0)).astype(d[k].dtype)
    return d
def setup_inputs_apart(rng):
    d = setup_inputs(rng)
    f = (10.0 ** rng.permutation(np.linspace(-1.5, 1.5, N))).astype(np.float32).reshape(N, 1, 1)
    for k in ("x", "a"): d[k] = (d[k].astype(np.float32) * f).astype(d[k].dtype)
    return d
def reference(x, a):
    X, A = x.astype(np.float64), a.astype(np.float64)
    y = np.zeros((N, 128, TK))
    for i in range(GR):
        for j in range(GC):
            t = sum(RA[i][k] * CB[j][l] * X[k * GC + l] for k in range(GR) for l in range(GC))
            y[i * GC + j] = A[i * GC + j].T @ t
    return {"y": y.astype(ml_dtypes.bfloat16)}

@@ -1,0 +1,113 @@
+from concourse.bass import DstId, RemoteDMATransfer
+from concourse.mybir import AluOpType
+
+W = 128
+G = 4
+
+SCRATCH = {
+    "xs": ("sbuf", [128, G * W], "bfloat16"),
+    "us": ("sbuf", [128, G * W], "bfloat16"),
+    "a1": ("sbuf", [128, W], "bfloat16"),
+    "ac": ("sbuf", [128, G * W], "bfloat16"),
+    "ct": ("sbuf", [128, G * W], "bfloat16"),
+    "zs": ("sbuf", [128, G * W + 1], "bfloat16"),
+    "dz": ("dram", [128 * (G * W + 1)], "bfloat16"),
+    "idn": ("sbuf", [128, G * W], "bfloat16"),
+    "yo": ("sbuf", [128, W], "bfloat16"),
+    "pu": ("psum", [128, 512], "float32"),
+    "py": ("psum", [128, 512], "float32"),
+}
+SEMAPHORES = (["sx", "sa", "smz", "smi", "smc", "sdz", "sid", "spu", "su", "ssa", "spy", "syo", "sst", "sl"]
+              + ["xa%d" % n for n in range(G)] + ["ua%d" % n for n in range(G)])
+
+
+def rank_program(g, core, T, topo):
+    rank = T.rank_of(core)
+    if rank is None:
+        return
+    RA, CB = T.tables["RA"], T.tables["CB"]
+    GC = len(CB)
+    GR = len(RA)
+    i, j = rank // GC, rank % GC
+    S = T.sem
+    te, ve = g.tensor, g.vector
+
+    def blk(t, n):
+        return t[:, n * W:(n + 1) * W]
+
+    def send(ap, dests, rsem):
+        m = topo.mask(core, dests[0])
+        for d in dests:
+            m &= topo.mask(core, d)
+        ids = []
+        for d in dests:
+            rid, pid = topo.addr(d, core)
+            ids.append(DstId(rid=rid, pnc=pid))
+        g.remote_dma_fused([RemoteDMATransfer(dst_ids=ids, dma_engine_mask=m, remote_sem=rsem,
+                                              srcs=[ap], dsts=[ap for _ in dests], alu_op=0)], local_sem=S.sl)
+        return bin(m).count("1")
+
+    cvals = sorted(set(CB[j]))
+    avals = sorted(set(RA[i]) - {1})
+    V = len(cvals)
+
+    g.sync.dma_start(blk(T.xs, j), T.x[:, :]).then_inc(S.sx, 16)
+    g.scalar.dma_start(T.a1[:, :], T.a[:, :]).then_inc(S.sa, 16)
+
+    L = V * W
+    ve.memset(T.zs[:, 0:L + 1], 0.0).then_inc(S.smz, 1)
+    ve.wait_ge(S.smz, 1)
+    for v, c in enumerate(cvals):
+        ve.memset(T.zs[:, v * W:v * W + 1], float(c)).then_inc(S.smi, 1)
+    g.scalar.wait_ge(S.smi, V)
+    g.scalar.dma_start(T.dz[0:128 * (L + 1)], T.zs[:, 0:L + 1]).then_inc(S.sdz, 16)
+    g.scalar.wait_ge(S.sdz, 16)
+    g.scalar.dma_start(T.idn[:, 0:L], T.dz[0:128 * L]).then_inc(S.sid, 16)
+
+    for v, c in enumerate(avals):
+        ve.memset(blk(T.ct, v), float(c)).then_inc(S.smc, 1)
+    if avals:
+        ve.wait_ge(S.smc, len(avals))
+        ve.wait_ge(S.sa, 16)
+    for v, c in enumerate(avals):
+        ve.tensor_tensor(blk(T.ac, v), T.a1[:, :], blk(T.ct, v), AluOpType.mult).then_inc(S.ssa, 1)
+
+    def a_times(c):
+        return T.a1[:, :] if c == 1 else blk(T.ac, avals.index(c))
+
+    g.wait_ge(S.sx, 16)
+    ne = send(blk(T.xs, j), [T.cores[i * GC + (j + d) % GC] for d in range(1, GC)], S["xa%d" % j])
+
+    te.wait_ge(S.sid, 16)
+    te.wait_ge(S.sx, 16)
+    order = [(j - d) % GC for d in range(GC)]
+    for n, l in enumerate(order):
+        if l != j:
+            te.wait_ge(S["xa%d" % l], ne)
+        mm = te.matmul(T.pu[:, 0:W], lhsT=blk(T.idn, cvals.index(CB[j][l])), rhs=blk(T.xs, l),
+                       start=(n == 0), stop=(n == GC - 1))
+    mm.then_inc(S.spu, 1)
+    ve.wait_ge(S.spu, 1)
+    ve.tensor_copy(blk(T.us, i), T.pu[:, 0:W]).then_inc(S.su, 1)
+
+    g.wait_ge(S.su, 1)
+    send(blk(T.us, i), [T.cores[((i + d) % GR) * GC + j] for d in range(1, GR)], S["ua%d" % i])
+
+    te.wait_ge(S.sa, 16)
+    if avals:
+        te.wait_ge(S.ssa, len(avals))
+    te.wait_ge(S.su, 1)
+    order = [(i - d) % GR for d in range(GR)]
+    for n, k in enumerate(order):
+        if k != i:
+            te.wait_ge(S["ua%d" % k], ne)
+        mm = te.matmul(T.py[:, 0:W], lhsT=a_times(RA[i][k]), rhs=blk(T.us, k),
+                       start=(n == 0), stop=(n == GR - 1))
+    mm.then_inc(S.spy, 1)
+    ve.wait_ge(S.spy, 1)
+    ve.tensor_copy(T.yo[:, :], T.py[:, 0:W]).then_inc(S.syo, 1)
+    g.sync.wait_ge(S.syo, 1)
+    g.sync.dma_start(T.y[:, :], T.yo[:, :]).then_inc(S.sst, 16)
+
+    g.wait_ge(S.sl, 2 * ne)
+    g.wait_ge(S.sst, 16)

@@ -2,22 +2,24 @@ from concourse.bass import DstId, RemoteDMATransfer
 from concourse.mybir import AluOpType
 
 W = 128
+H = W // 2
 G = 4
 
 SCRATCH = {
+    "xd": ("dram", [128, W], "bfloat16"),
     "xs": ("sbuf", [128, G * W], "bfloat16"),
     "us": ("sbuf", [128, G * W], "bfloat16"),
     "a1": ("sbuf", [128, W], "bfloat16"),
     "ac": ("sbuf", [128, G * W], "bfloat16"),
-    "ct": ("sbuf", [128, G * W], "bfloat16"),
-    "zs": ("sbuf", [128, G * W + 1], "bfloat16"),
-    "dz": ("dram", [128 * (G * W + 1)], "bfloat16"),
+    "on": ("sbuf", [128, W], "bfloat16"),
+    "i1": ("sbuf", [128, W], "bfloat16"),
     "idn": ("sbuf", [128, G * W], "bfloat16"),
     "yo": ("sbuf", [128, W], "bfloat16"),
     "pu": ("psum", [128, 512], "float32"),
-    "py": ("psum", [128, 512], "float32"),
+    "py0": ("psum", [128, 512], "float32"),
+    "py1": ("psum", [128, 512], "float32"),
 }
-SEMAPHORES = (["sx", "sa", "smz", "smi", "smc", "sdz", "sid", "spu", "su", "ssa", "spy", "syo", "sst", "sl"]
+SEMAPHORES = (["sxd", "sx", "sa", "smz", "si1", "sid", "spu", "su", "ssa", "spy0", "spy1", "syo", "sst", "sl"]
               + ["xa%d" % n for n in range(G)] + ["ua%d" % n for n in range(G)])
 
 
@@ -35,7 +37,7 @@ def rank_program(g, core, T, topo):
     def blk(t, n):
         return t[:, n * W:(n + 1) * W]
 
-    def send(ap, dests, rsem):
+    def send(src, dst, dests, rsem):
         m = topo.mask(core, dests[0])
         for d in dests:
             m &= topo.mask(core, d)
@@ -44,69 +46,79 @@ def rank_program(g, core, T, topo):
             rid, pid = topo.addr(d, core)
             ids.append(DstId(rid=rid, pnc=pid))
         g.remote_dma_fused([RemoteDMATransfer(dst_ids=ids, dma_engine_mask=m, remote_sem=rsem,
-                                              srcs=[ap], dsts=[ap for _ in dests], alu_op=0)], local_sem=S.sl)
+                                              srcs=[src], dsts=[dst for _ in dests], alu_op=0)], local_sem=S.sl)
         return bin(m).count("1")
 
-    cvals = sorted(set(CB[j]))
-    avals = sorted(set(RA[i]) - {1})
-    V = len(cvals)
+    xorder = [(j - d) % GC for d in range(GC)]
+    last = xorder[-1]
+    c = CB[j][last]
+    dw = {l: CB[j][l] / c for l in xorder[:-1]}
+    aw = [RA[i][k] * c for k in range(GR)]
+    dvals = sorted(set(dw.values()) - {1})
+    avals = sorted(set(aw) - {1})
 
+    g.sync.dma_start(T.xd[:, :], T.x[:, :]).then_inc(S.sxd, 16)
     g.sync.dma_start(blk(T.xs, j), T.x[:, :]).then_inc(S.sx, 16)
-    g.scalar.dma_start(T.a1[:, :], T.a[:, :]).then_inc(S.sa, 16)
+    g.sync.dma_start(T.a1[:, :], T.a[:, :]).then_inc(S.sa, 16)
 
-    L = V * W
-    ve.memset(T.zs[:, 0:L + 1], 0.0).then_inc(S.smz, 1)
-    ve.wait_ge(S.smz, 1)
-    for v, c in enumerate(cvals):
-        ve.memset(T.zs[:, v * W:v * W + 1], float(c)).then_inc(S.smi, 1)
-    g.scalar.wait_ge(S.smi, V)
-    g.scalar.dma_start(T.dz[0:128 * (L + 1)], T.zs[:, 0:L + 1]).then_inc(S.sdz, 16)
-    g.scalar.wait_ge(S.sdz, 16)
-    g.scalar.dma_start(T.idn[:, 0:L], T.dz[0:128 * L]).then_inc(S.sid, 16)
+    ve.memset(T.on[:, :], 1.0).then_inc(S.smz, 1)
+    g.wait_ge(S.sxd, 16)
+    ne = send(T.xd[:, :], blk(T.xs, j), [T.cores[i * GC + (j + d) % GC] for d in range(1, GC)], S["xa%d" % j])
 
-    for v, c in enumerate(avals):
-        ve.memset(blk(T.ct, v), float(c)).then_inc(S.smc, 1)
+    g.wait_ge(S.smz, 1)
+    g.affine_select(out=T.i1[:, :], in_=T.on[:, :], pattern=[[-1, W]], compare_op=AluOpType.is_equal, fill=0.0,
+                    base=0, channel_multiplier=1).then_inc(S.si1, 1)
+
     if avals:
-        ve.wait_ge(S.smc, len(avals))
         ve.wait_ge(S.sa, 16)
-    for v, c in enumerate(avals):
-        ve.tensor_tensor(blk(T.ac, v), T.a1[:, :], blk(T.ct, v), AluOpType.mult).then_inc(S.ssa, 1)
+    for v, w in enumerate(avals):
+        ve.tensor_scalar(blk(T.ac, v), T.a1[:, :], float(w), None, AluOpType.mult).then_inc(S.ssa, 1)
+    if dvals:
+        ve.wait_ge(S.si1, 1)
+    for v, w in enumerate(dvals):
+        ve.tensor_scalar(blk(T.idn, v), T.i1[:, :], float(w), None, AluOpType.mult).then_inc(S.sid, 1)
 
-    def a_times(c):
-        return T.a1[:, :] if c == 1 else blk(T.ac, avals.index(c))
+    def a_times(w):
+        return T.a1[:, :] if w == 1 else blk(T.ac, avals.index(w))
 
-    g.wait_ge(S.sx, 16)
-    ne = send(blk(T.xs, j), [T.cores[i * GC + (j + d) % GC] for d in range(1, GC)], S["xa%d" % j])
+    def i_times(w):
+        return T.i1[:, :] if w == 1 else blk(T.idn, dvals.index(w))
 
-    te.wait_ge(S.sid, 16)
+    te.wait_ge(S.si1, 1)
+    if dvals:
+        te.wait_ge(S.sid, len(dvals))
     te.wait_ge(S.sx, 16)
-    order = [(j - d) % GC for d in range(GC)]
-    for n, l in enumerate(order):
+    for n, l in enumerate(xorder[:-1]):
         if l != j:
             te.wait_ge(S["xa%d" % l], ne)
-        mm = te.matmul(T.pu[:, 0:W], lhsT=blk(T.idn, cvals.index(CB[j][l])), rhs=blk(T.xs, l),
-                       start=(n == 0), stop=(n == GC - 1))
+        mm = te.matmul(T.pu[:, 0:W], lhsT=i_times(dw[l]), rhs=blk(T.xs, l), start=(n == 0), stop=(n == GC - 2))
     mm.then_inc(S.spu, 1)
     ve.wait_ge(S.spu, 1)
-    ve.tensor_copy(blk(T.us, i), T.pu[:, 0:W]).then_inc(S.su, 1)
+    ve.wait_ge(S["xa%d" % last], ne)
+    ve.tensor_tensor(blk(T.us, i), T.pu[:, 0:W], blk(T.xs, last), AluOpType.add).then_inc(S.su, 1)
 
     g.wait_ge(S.su, 1)
-    send(blk(T.us, i), [T.cores[((i + d) % GR) * GC + j] for d in range(1, GR)], S["ua%d" % i])
+    send(blk(T.us, i), blk(T.us, i), [T.cores[((i + d) % GR) * GC + j] for d in range(1, GR)], S["ua%d" % i])
 
     te.wait_ge(S.sa, 16)
     if avals:
         te.wait_ge(S.ssa, len(avals))
     te.wait_ge(S.su, 1)
-    order = [(i - d) % GR for d in range(GR)]
-    for n, k in enumerate(order):
+    korder = [(i - d) % GR for d in range(GR)]
+    for n, k in enumerate(korder):
         if k != i:
             te.wait_ge(S["ua%d" % k], ne)
-        mm = te.matmul(T.py[:, 0:W], lhsT=a_times(RA[i][k]), rhs=blk(T.us, k),
+        m0 = te.matmul(T.py0[:, 0:H], lhsT=a_times(aw[k]), rhs=T.us[:, k * W:k * W + H],
                        start=(n == 0), stop=(n == GR - 1))
-    mm.then_inc(S.spy, 1)
-    ve.wait_ge(S.spy, 1)
-    ve.tensor_copy(T.yo[:, :], T.py[:, 0:W]).then_inc(S.syo, 1)
-    g.sync.wait_ge(S.syo, 1)
+        m1 = te.matmul(T.py1[:, 0:H], lhsT=a_times(aw[k]), rhs=T.us[:, k * W + H:(k + 1) * W],
+                       start=(n == 0), stop=(n == GR - 1))
+    m0.then_inc(S.spy0, 1)
+    m1.then_inc(S.spy1, 1)
+    ve.wait_ge(S.spy0, 1)
+    ve.tensor_copy(T.yo[:, 0:H], T.py0[:, 0:H]).then_inc(S.syo, 1)
+    ve.wait_ge(S.spy1, 1)
+    ve.tensor_copy(T.yo[:, H:W], T.py1[:, 0:H]).then_inc(S.syo, 1)
+    g.sync.wait_ge(S.syo, 2)
     g.sync.dma_start(T.y[:, :], T.yo[:, :]).then_inc(S.sst, 16)
 
     g.wait_ge(S.sl, 2 * ne)

from concourse.bass import DstId, RemoteDMATransfer
from concourse.mybir import AluOpType

W = 128
H = W // 2
G = 4

SCRATCH = {
    "xd": ("dram", [128, W], "bfloat16"),
    "xs": ("sbuf", [128, G * W], "bfloat16"),
    "us": ("sbuf", [128, G * W], "bfloat16"),
    "a1": ("sbuf", [128, W], "bfloat16"),
    "ac": ("sbuf", [128, G * W], "bfloat16"),
    "on": ("sbuf", [128, W], "bfloat16"),
    "i1": ("sbuf", [128, W], "bfloat16"),
    "idn": ("sbuf", [128, G * W], "bfloat16"),
    "yo": ("sbuf", [128, W], "bfloat16"),
    "pu": ("psum", [128, 512], "float32"),
    "py0": ("psum", [128, 512], "float32"),
    "py1": ("psum", [128, 512], "float32"),
}
SEMAPHORES = (["sxd", "sx", "sa", "smz", "si1", "sid", "spu", "su", "ssa", "spy0", "spy1", "syo", "sst", "sl"]
              + ["xa%d" % n for n in range(G)] + ["ua%d" % n for n in range(G)])


def rank_program(g, core, T, topo):
    rank = T.rank_of(core)
    if rank is None:
        return
    RA, CB = T.tables["RA"], T.tables["CB"]
    GC = len(CB)
    GR = len(RA)
    i, j = rank // GC, rank % GC
    S = T.sem
    te, ve = g.tensor, g.vector

    def blk(t, n):
        return t[:, n * W:(n + 1) * W]

    def send(src, dst, dests, rsem):
        m = topo.mask(core, dests[0])
        for d in dests:
            m &= topo.mask(core, d)
        ids = []
        for d in dests:
            rid, pid = topo.addr(d, core)
            ids.append(DstId(rid=rid, pnc=pid))
        g.remote_dma_fused([RemoteDMATransfer(dst_ids=ids, dma_engine_mask=m, remote_sem=rsem,
                                              srcs=[src], dsts=[dst for _ in dests], alu_op=0)], local_sem=S.sl)
        return bin(m).count("1")

    xorder = [(j - d) % GC for d in range(GC)]
    last = xorder[-1]
    c = CB[j][last]
    dw = {l: CB[j][l] / c for l in xorder[:-1]}
    aw = [RA[i][k] * c for k in range(GR)]
    dvals = sorted(set(dw.values()) - {1})
    avals = sorted(set(aw) - {1})

    g.sync.dma_start(T.xd[:, :], T.x[:, :]).then_inc(S.sxd, 16)
    g.sync.dma_start(blk(T.xs, j), T.x[:, :]).then_inc(S.sx, 16)
    g.sync.dma_start(T.a1[:, :], T.a[:, :]).then_inc(S.sa, 16)

    ve.memset(T.on[:, :], 1.0).then_inc(S.smz, 1)
    g.wait_ge(S.sxd, 16)
    ne = send(T.xd[:, :], blk(T.xs, j), [T.cores[i * GC + (j + d) % GC] for d in range(1, GC)], S["xa%d" % j])

    g.wait_ge(S.smz, 1)
    g.affine_select(out=T.i1[:, :], in_=T.on[:, :], pattern=[[-1, W]], compare_op=AluOpType.is_equal, fill=0.0,
                    base=0, channel_multiplier=1).then_inc(S.si1, 1)

    if avals:
        ve.wait_ge(S.sa, 16)
    for v, w in enumerate(avals):
        ve.tensor_scalar(blk(T.ac, v), T.a1[:, :], float(w), None, AluOpType.mult).then_inc(S.ssa, 1)
    if dvals:
        ve.wait_ge(S.si1, 1)
    for v, w in enumerate(dvals):
        ve.tensor_scalar(blk(T.idn, v), T.i1[:, :], float(w), None, AluOpType.mult).then_inc(S.sid, 1)

    def a_times(w):
        return T.a1[:, :] if w == 1 else blk(T.ac, avals.index(w))

    def i_times(w):
        return T.i1[:, :] if w == 1 else blk(T.idn, dvals.index(w))

    te.wait_ge(S.si1, 1)
    if dvals:
        te.wait_ge(S.sid, len(dvals))
    te.wait_ge(S.sx, 16)
    for n, l in enumerate(xorder[:-1]):
        if l != j:
            te.wait_ge(S["xa%d" % l], ne)
        mm = te.matmul(T.pu[:, 0:W], lhsT=i_times(dw[l]), rhs=blk(T.xs, l), start=(n == 0), stop=(n == GC - 2))
    mm.then_inc(S.spu, 1)
    ve.wait_ge(S.spu, 1)
    ve.wait_ge(S["xa%d" % last], ne)
    ve.tensor_tensor(blk(T.us, i), T.pu[:, 0:W], blk(T.xs, last), AluOpType.add).then_inc(S.su, 1)

    g.wait_ge(S.su, 1)
    send(blk(T.us, i), blk(T.us, i), [T.cores[((i + d) % GR) * GC + j] for d in range(1, GR)], S["ua%d" % i])

    te.wait_ge(S.sa, 16)
    if avals:
        te.wait_ge(S.ssa, len(avals))
    te.wait_ge(S.su, 1)
    korder = [(i - d) % GR for d in range(GR)]
    for n, k in enumerate(korder):
        if k != i:
            te.wait_ge(S["ua%d" % k], ne)
        m0 = te.matmul(T.py0[:, 0:H], lhsT=a_times(aw[k]), rhs=T.us[:, k * W:k * W + H],
                       start=(n == 0), stop=(n == GR - 1))
        m1 = te.matmul(T.py1[:, 0:H], lhsT=a_times(aw[k]), rhs=T.us[:, k * W + H:(k + 1) * W],
                       start=(n == 0), stop=(n == GR - 1))
    m0.then_inc(S.spy0, 1)
    m1.then_inc(S.spy1, 1)
    ve.wait_ge(S.spy0, 1)
    ve.tensor_copy(T.yo[:, 0:H], T.py0[:, 0:H]).then_inc(S.syo, 1)
    ve.wait_ge(S.spy1, 1)
    ve.tensor_copy(T.yo[:, H:W], T.py1[:, 0:H]).then_inc(S.syo, 1)
    g.sync.wait_ge(S.syo, 2)
    g.sync.dma_start(T.y[:, :], T.yo[:, :]).then_inc(S.sst, 16)

    g.wait_ge(S.sl, 2 * ne)
    g.wait_ge(S.sst, 16)
